import numpy as np
import ml_dtypes


def mxq(x, axis, fmt="e4m3"):
    dtype, down = {"e4m3": (ml_dtypes.float8_e4m3fn, 7), "e5m2": (ml_dtypes.float8_e5m2, 14)}[fmt]
    v = np.moveaxis(np.asarray(x, np.float32).astype(ml_dtypes.bfloat16).astype(np.float64), axis, -1)
    blocks = v.reshape(v.shape[:-1] + (-1, 32))
    amax = np.abs(blocks).max(-1, keepdims=True)
    byte = np.maximum(np.where(amax > 0, np.frexp(amax)[1] - 1 + 127, 0) - down, 1)
    scale = np.exp2(byte - 127.0)
    codes = (blocks / scale).astype(np.float32).astype(dtype).astype(np.float64)
    return np.moveaxis((codes * scale).reshape(v.shape), -1, axis)


WIDE = False


def mx_kscale(k, group=512):
    if not WIDE:
        return np.ones(k)
    levels = np.array([18, -18])
    if group != 512:
        return np.exp2(np.random.permutation(np.resize(levels, k // group))).repeat(group)
    if k % 512:
        return np.exp2(np.random.permutation(np.resize(levels, k // 32))).repeat(32)
    a = np.empty((k // 512, 16))
    for p in range(k // 512):
        a[p, :8] = np.random.permutation(np.resize(levels, 8))
        for g in range(8):
            far = levels[np.abs(levels - a[p, g]) >= 10]
            a[p, g + 8] = far[np.random.randint(len(far))]
    return np.exp2(a.ravel()).repeat(32)


def f64(x):
    return np.asarray(x).astype(np.float64)


G, D, M, N = 4, 128, 128, 512


def setup_inputs():
    n = np.random.standard_normal
    s_d = mx_kscale(D, 0)
    return {
        "dy": (n((G, D, N)) * s_d[:, None]).astype(np.float32),
        "w": (n((G, D, M)) / np.sqrt(D) / s_d[:, None]).astype(np.float32),
        "sg": (1 / (1 + np.exp(-n((G, M, N))))).astype(np.float32),
        "xg": (n((G, M, N))).astype(np.float32),
    }


def reference(dy, w, sg, xg):
    wq = mxq(f64(w), 1, "e5m2")
    dyq = mxq(f64(dy), 1, "e5m2")
    z = wq.transpose(0, 2, 1) @ dyq
    y = z * f64(xg) * f64(sg) * (1.0 - f64(sg))
    return y

@@ -1,0 +1,109 @@
+from contextlib import ExitStack
+
+import concourse.mybir as mybir
+
+G, D, M, N = 4, 128, 128, 512
+FLOPS = 2 * G * D * M * N
+
+F32 = mybir.dt.float32
+BF16 = mybir.dt.bfloat16
+U32 = mybir.dt.uint32
+U8 = mybir.dt.uint8
+E5M2X4 = mybir.dt.float8_e5m2_x4
+ALU = mybir.AluOpType
+
+P = 128
+PACK = 4
+ROWS = D // PACK
+HALF = N // 2
+
+
+def tile_rows_gback_sig_kernel(tc, dy, w, sg, xg, out):
+    nc = tc.nc
+    with ExitStack() as ctx:
+        sb = ctx.enter_context(tc.tile_pool(name="sb", bufs=1))
+        ps = ctx.enter_context(tc.psum_pool(name="ps", bufs=1))
+        ctx.enter_context(tc.manual_schedule())
+
+        w_rows = w.rearrange("g (p j) m -> (g p) j m", j=PACK)
+        dy_rows = dy.rearrange("g (p j) n -> (g p) j n", j=PACK)
+
+        w_raw = sb.tile([P, PACK, M], F32, name="w_raw", align_bytes=64)
+        dy_raw = [sb.tile([P, PACK, HALF], F32, name="dy_raw%d" % h, align_bytes=64) for h in range(2)]
+        w_bf = sb.tile([P, M, PACK], BF16, name="w_bf", align_bytes=64)
+        dy_bf = [sb.tile([P, HALF, PACK], BF16, name="dy_bf%d" % h, align_bytes=64) for h in range(2)]
+        w_codes = sb.tile([P, M], U32, name="w_codes", align_bytes=64)
+        w_scales = sb.tile([P, M], U8, name="w_scales", align_bytes=64)
+        dy_codes = sb.tile([P, N], U32, name="dy_codes", align_bytes=64)
+        dy_scales = sb.tile([P, N], U8, name="dy_scales", align_bytes=64)
+        gate = [sb.tile([P, N], F32, name="gate%d" % g, align_bytes=64) for g in range(G)]
+        gated = [sb.tile([P, N], F32, name="gated%d" % g, align_bytes=64) for g in range(G)]
+        slope = [sb.tile([P, N], F32, name="slope%d" % g, align_bytes=64) for g in range(G)]
+        factor = [sb.tile([P, N], F32, name="factor%d" % g, align_bytes=64) for g in range(G)]
+        result = [sb.tile([P, N], F32, name="result%d" % g, align_bytes=64) for g in range(G)]
+        z = [ps.tile([P, N], F32, name="z%d" % g) for g in range(G)]
+
+        nc.sync.dma_start(out=w_raw[:], in_=w_rows)
+        for h in range(2):
+            nc.sync.dma_start(out=dy_raw[h][:], in_=dy_rows[:, :, h * HALF : (h + 1) * HALF])
+        for g in range(G):
+            nc.sync.dma_start(out=gate[g][:], in_=sg[g])
+            nc.sync.dma_start(out=gated[g][:], in_=xg[g])
+
+        def interleave(copy, dst, src, cols):
+            copy(
+                out=dst[:, cols, :].rearrange("p (c i) j -> p c j i", i=4),
+                in_=src[:, :, cols].rearrange("p j (c i) -> p c j i", i=4),
+            )
+
+        def quantize(codes, scales, src):
+            nc.vector.quantize_mx(
+                out=codes.bitcast(E5M2X4), scales=scales, in_=src[:].rearrange("p c j -> p (c j)")
+            )
+
+        def make_slope(g):
+            nc.vector.scalar_tensor_tensor(
+                out=slope[g][:], in0=gate[g][:], scalar=1.0, in1=gate[g][:], op0=ALU.subtract, op1=ALU.mult
+            )
+
+        def make_factor(g, cols):
+            nc.vector.tensor_tensor(out=factor[g][:, cols], in0=slope[g][:, cols], in1=gated[g][:, cols], op=ALU.mult)
+
+        def finish(g, cols):
+            nc.vector.scalar_tensor_tensor(
+                out=result[g][:, cols], in0=z[g][:, cols], scalar=-1.0, in1=factor[g][:, cols], op0=ALU.mult, op1=ALU.mult
+            )
+            nc.sync.dma_start(out=out[g][:, cols], in_=result[g][:, cols])
+
+        whole = slice(0, N)
+        halves = [slice(0, HALF), slice(HALF, N)]
+
+        interleave(nc.scalar.copy, w_bf, w_raw, slice(0, M))
+        interleave(nc.vector.tensor_copy, dy_bf[0], dy_raw[0], slice(0, HALF))
+        quantize(dy_codes[:, halves[0]], dy_scales[:, halves[0]], dy_bf[0])
+        interleave(nc.vector.tensor_copy, dy_bf[1], dy_raw[1], slice(0, 160))
+        interleave(nc.scalar.copy, dy_bf[1], dy_raw[1], slice(160, HALF))
+        quantize(w_codes[:], w_scales[:], w_bf)
+        make_slope(0)
+        quantize(dy_codes[:, halves[1]], dy_scales[:, halves[1]], dy_bf[1])
+
+        for g in range(G):
+            rows = slice(ROWS * g, ROWS * (g + 1))
+            nc.tensor.matmul_mx(
+                out=z[g][:],
+                lhsT=w_codes[rows, :].bitcast(E5M2X4),
+                lhsT_scale=w_scales[rows, :],
+                rhs=dy_codes[rows, :].bitcast(E5M2X4),
+                rhs_scale=dy_scales[rows, :],
+                start=True,
+                stop=True,
+            )
+
+        for g in range(G - 1):
+            make_factor(g, whole)
+            make_slope(g + 1)
+            finish(g, whole)
+        for cols in halves:
+            make_factor(G - 1, cols)
+        for cols in halves:
+            finish(G - 1, cols)

@@ -36,19 +36,40 @@ def tile_rows_gback_sig_kernel(tc, dy, w, sg, xg, out):
         w_scales = sb.tile([P, M], U8, name="w_scales", align_bytes=64)
         dy_codes = sb.tile([P, N], U32, name="dy_codes", align_bytes=64)
         dy_scales = sb.tile([P, N], U8, name="dy_scales", align_bytes=64)
-        gate = [sb.tile([P, N], F32, name="gate%d" % g, align_bytes=64) for g in range(G)]
-        gated = [sb.tile([P, N], F32, name="gated%d" % g, align_bytes=64) for g in range(G)]
-        slope = [sb.tile([P, N], F32, name="slope%d" % g, align_bytes=64) for g in range(G)]
-        factor = [sb.tile([P, N], F32, name="factor%d" % g, align_bytes=64) for g in range(G)]
-        result = [sb.tile([P, N], F32, name="result%d" % g, align_bytes=64) for g in range(G)]
-        z = [ps.tile([P, N], F32, name="z%d" % g) for g in range(G)]
+        def pair_tiles(label):
+            return [
+                [sb.tile([P, 2, HALF], F32, name="%s%d%d" % (label, h, q), align_bytes=64) for q in range(2)]
+                for h in range(2)
+            ]
+
+        gate = pair_tiles("gate")
+        gated = pair_tiles("gated")
+        slope = pair_tiles("slope")
+        partial = pair_tiles("partial")
+        result = pair_tiles("result")
+        z = [[ps.tile([P, N], F32, name="z%d%d" % (h, g)) for g in range(G)] for h in range(2)]
+        halves = [slice(0, HALF), slice(HALF, N)]
+
+        def pair_rows(dram, h, q):
+            return dram[2 * q : 2 * q + 2, :, halves[h]].rearrange("g m n -> m g n")
+
+        def load_dy(h):
+            nc.sync.dma_start(out=dy_raw[h][:], in_=dy_rows[:, :, halves[h]])
+
+        def load_pair(tiles, dram, h, q):
+            nc.sync.dma_start(out=tiles[h][q][:], in_=pair_rows(dram, h, q))
 
         nc.sync.dma_start(out=w_raw[:], in_=w_rows)
-        for h in range(2):
-            nc.sync.dma_start(out=dy_raw[h][:], in_=dy_rows[:, :, h * HALF : (h + 1) * HALF])
-        for g in range(G):
-            nc.sync.dma_start(out=gate[g][:], in_=sg[g])
-            nc.sync.dma_start(out=gated[g][:], in_=xg[g])
+        load_dy(0)
+        load_pair(gate, sg, 0, 0)
+        load_pair(gate, sg, 0, 1)
+        load_dy(1)
+        load_pair(gated, xg, 0, 0)
+        load_pair(gated, xg, 0, 1)
+        load_pair(gate, sg, 1, 0)
+        load_pair(gate, sg, 1, 1)
+        load_pair(gated, xg, 1, 0)
+        load_pair(gated, xg, 1, 1)
 
         def interleave(copy, dst, src, cols):
             copy(
@@ -61,49 +82,66 @@ def tile_rows_gback_sig_kernel(tc, dy, w, sg, xg, out):
                 out=codes.bitcast(E5M2X4), scales=scales, in_=src[:].rearrange("p c j -> p (c j)")
             )
 
-        def make_slope(g):
+        def multiply(h):
+            for g in range(G):
+                rows = slice(ROWS * g, ROWS * (g + 1))
+                nc.tensor.matmul_mx(
+                    out=z[h][g][:],
+                    lhsT=w_codes[rows, :].bitcast(E5M2X4),
+                    lhsT_scale=w_scales[rows, :],
+                    rhs=dy_codes[rows, :].bitcast(E5M2X4),
+                    rhs_scale=dy_scales[rows, :],
+                    start=True,
+                    stop=True,
+                )
+
+        def flat(t):
+            return t[:].rearrange("p g n -> p (g n)")
+
+        def make_slope(h, q):
             nc.vector.scalar_tensor_tensor(
-                out=slope[g][:], in0=gate[g][:], scalar=1.0, in1=gate[g][:], op0=ALU.subtract, op1=ALU.mult
+                out=flat(slope[h][q]), in0=flat(gate[h][q]), scalar=1.0, in1=flat(gate[h][q]),
+                op0=ALU.subtract, op1=ALU.mult,
             )
 
-        def make_factor(g, cols):
-            nc.vector.tensor_tensor(out=factor[g][:, cols], in0=slope[g][:, cols], in1=gated[g][:, cols], op=ALU.mult)
-
-        def finish(g, cols):
-            nc.vector.scalar_tensor_tensor(
-                out=result[g][:, cols], in0=z[g][:, cols], scalar=-1.0, in1=factor[g][:, cols], op0=ALU.mult, op1=ALU.mult
+        def times_gated(h, q, members):
+            nc.vector.tensor_tensor(
+                out=result[h][q][:, members, :], in0=partial[h][q][:, members, :], in1=gated[h][q][:, members, :],
+                op=ALU.mult,
             )
-            nc.sync.dma_start(out=out[g][:, cols], in_=result[g][:, cols])
+            nc.sync.dma_start(out=pair_rows(out, h, q)[:, members, :], in_=result[h][q][:, members, :])
 
-        whole = slice(0, N)
-        halves = [slice(0, HALF), slice(HALF, N)]
+        def times_sums(dst, src, h, g):
+            q, i = divmod(g, 2)
+            nc.vector.scalar_tensor_tensor(
+                out=dst[h][q][:, i, :], in0=z[h][g][:, halves[h]], scalar=-1.0, in1=src[h][q][:, i, :],
+                op0=ALU.mult, op1=ALU.mult,
+            )
 
+        nc.vector.memset(dy_codes[:, halves[1]], 0)
+        nc.vector.memset(dy_scales[:, halves[1]].bitcast(U32), 0)
         interleave(nc.scalar.copy, w_bf, w_raw, slice(0, M))
-        interleave(nc.vector.tensor_copy, dy_bf[0], dy_raw[0], slice(0, HALF))
-        quantize(dy_codes[:, halves[0]], dy_scales[:, halves[0]], dy_bf[0])
-        interleave(nc.vector.tensor_copy, dy_bf[1], dy_raw[1], slice(0, 160))
-        interleave(nc.scalar.copy, dy_bf[1], dy_raw[1], slice(160, HALF))
         quantize(w_codes[:], w_scales[:], w_bf)
-        make_slope(0)
-        quantize(dy_codes[:, halves[1]], dy_scales[:, halves[1]], dy_bf[1])
+        interleave(nc.vector.tensor_copy, dy_bf[0], dy_raw[0], slice(0, 144))
+        interleave(nc.scalar.copy, dy_bf[0], dy_raw[0], slice(144, HALF))
+        quantize(dy_codes[:, halves[0]], dy_scales[:, halves[0]], dy_bf[0])
+        multiply(0)
+        interleave(nc.scalar.copy, dy_bf[1], dy_raw[1], slice(0, HALF))
 
+        for q in range(2):
+            make_slope(0, q)
         for g in range(G):
-            rows = slice(ROWS * g, ROWS * (g + 1))
-            nc.tensor.matmul_mx(
-                out=z[g][:],
-                lhsT=w_codes[rows, :].bitcast(E5M2X4),
-                lhsT_scale=w_scales[rows, :],
-                rhs=dy_codes[rows, :].bitcast(E5M2X4),
-                rhs_scale=dy_scales[rows, :],
-                start=True,
-                stop=True,
-            )
+            times_sums(partial, slope, 0, g)
+        times_gated(0, 0, slice(0, 2))
+        quantize(dy_codes[:, halves[1]], dy_scales[:, halves[1]], dy_bf[1])
+        multiply(1)
+        times_gated(0, 1, slice(0, 2))
 
+        for q in range(2):
+            make_slope(1, q)
         for g in range(G - 1):
-            make_factor(g, whole)
-            make_slope(g + 1)
-            finish(g, whole)
-        for cols in halves:
-            make_factor(G - 1, cols)
-        for cols in halves:
-            finish(G - 1, cols)
+            times_sums(partial, slope, 1, g)
+        times_gated(1, 0, slice(0, 2))
+        times_sums(partial, slope, 1, G - 1)
+        times_gated(1, 1, slice(0, 1))
+        times_gated(1, 1, slice(1, 2))

@@ -16,6 +16,7 @@ P = 128
 PACK = 4
 ROWS = D // PACK
 HALF = N // 2
+QUARTER = N // 4
 
 
 def tile_rows_gback_sig_kernel(tc, dy, w, sg, xg, out):
@@ -29,9 +30,9 @@ def tile_rows_gback_sig_kernel(tc, dy, w, sg, xg, out):
         dy_rows = dy.rearrange("g (p j) n -> (g p) j n", j=PACK)
 
         w_raw = sb.tile([P, PACK, M], F32, name="w_raw", align_bytes=64)
-        dy_raw = [sb.tile([P, PACK, HALF], F32, name="dy_raw%d" % h, align_bytes=64) for h in range(2)]
+        dy_raw = [sb.tile([P, PACK, QUARTER], F32, name="dy_raw%d" % c, align_bytes=64) for c in range(4)]
         w_bf = sb.tile([P, M, PACK], BF16, name="w_bf", align_bytes=64)
-        dy_bf = [sb.tile([P, HALF, PACK], BF16, name="dy_bf%d" % h, align_bytes=64) for h in range(2)]
+        dy_bf = [sb.tile([P, QUARTER, PACK], BF16, name="dy_bf%d" % c, align_bytes=64) for c in range(4)]
         w_codes = sb.tile([P, M], U32, name="w_codes", align_bytes=64)
         w_scales = sb.tile([P, M], U8, name="w_scales", align_bytes=64)
         dy_codes = sb.tile([P, N], U32, name="dy_codes", align_bytes=64)
@@ -53,17 +54,21 @@ def tile_rows_gback_sig_kernel(tc, dy, w, sg, xg, out):
         def pair_rows(dram, h, q):
             return dram[2 * q : 2 * q + 2, :, halves[h]].rearrange("g m n -> m g n")
 
-        def load_dy(h):
-            nc.sync.dma_start(out=dy_raw[h][:], in_=dy_rows[:, :, halves[h]])
+        quarters = [slice(c * QUARTER, (c + 1) * QUARTER) for c in range(4)]
+
+        def load_dy(c):
+            nc.sync.dma_start(out=dy_raw[c][:], in_=dy_rows[:, :, quarters[c]])
 
         def load_pair(tiles, dram, h, q):
             nc.sync.dma_start(out=tiles[h][q][:], in_=pair_rows(dram, h, q))
 
         nc.sync.dma_start(out=w_raw[:], in_=w_rows)
         load_dy(0)
+        load_dy(1)
         load_pair(gate, sg, 0, 0)
         load_pair(gate, sg, 0, 1)
-        load_dy(1)
+        load_dy(2)
+        load_dy(3)
         load_pair(gated, xg, 0, 0)
         load_pair(gated, xg, 0, 1)
         load_pair(gate, sg, 1, 0)
@@ -81,6 +86,9 @@ def tile_rows_gback_sig_kernel(tc, dy, w, sg, xg, out):
             nc.vector.quantize_mx(
                 out=codes.bitcast(E5M2X4), scales=scales, in_=src[:].rearrange("p c j -> p (c j)")
             )
+
+        def quantize_dy(c):
+            quantize(dy_codes[:, quarters[c]], dy_scales[:, quarters[c]], dy_bf[c])
 
         def multiply(h):
             for g in range(G):
@@ -121,19 +129,23 @@ def tile_rows_gback_sig_kernel(tc, dy, w, sg, xg, out):
         nc.vector.memset(dy_codes[:, halves[1]], 0)
         nc.vector.memset(dy_scales[:, halves[1]].bitcast(U32), 0)
         interleave(nc.scalar.copy, w_bf, w_raw, slice(0, M))
+        interleave(nc.vector.tensor_copy, dy_bf[0], dy_raw[0], slice(0, QUARTER))
         quantize(w_codes[:], w_scales[:], w_bf)
-        interleave(nc.vector.tensor_copy, dy_bf[0], dy_raw[0], slice(0, 144))
-        interleave(nc.scalar.copy, dy_bf[0], dy_raw[0], slice(144, HALF))
-        quantize(dy_codes[:, halves[0]], dy_scales[:, halves[0]], dy_bf[0])
+        quantize_dy(0)
+        interleave(nc.vector.tensor_copy, dy_bf[1], dy_raw[1], slice(0, 72))
+        interleave(nc.scalar.copy, dy_bf[1], dy_raw[1], slice(72, QUARTER))
+        quantize_dy(1)
         multiply(0)
-        interleave(nc.scalar.copy, dy_bf[1], dy_raw[1], slice(0, HALF))
+        for c in (2, 3):
+            interleave(nc.scalar.copy, dy_bf[c], dy_raw[c], slice(0, QUARTER))
 
         for q in range(2):
             make_slope(0, q)
         for g in range(G):
             times_sums(partial, slope, 0, g)
+        quantize_dy(2)
         times_gated(0, 0, slice(0, 2))
-        quantize(dy_codes[:, halves[1]], dy_scales[:, halves[1]], dy_bf[1])
+        quantize_dy(3)
         multiply(1)
         times_gated(0, 1, slice(0, 2))
 

from contextlib import ExitStack

import concourse.mybir as mybir

G, D, M, N = 4, 128, 128, 512
FLOPS = 2 * G * D * M * N

F32 = mybir.dt.float32
BF16 = mybir.dt.bfloat16
U32 = mybir.dt.uint32
U8 = mybir.dt.uint8
E5M2X4 = mybir.dt.float8_e5m2_x4
ALU = mybir.AluOpType

P = 128
PACK = 4
ROWS = D // PACK
HALF = N // 2
QUARTER = N // 4


def tile_rows_gback_sig_kernel(tc, dy, w, sg, xg, out):
    nc = tc.nc
    with ExitStack() as ctx:
        sb = ctx.enter_context(tc.tile_pool(name="sb", bufs=1))
        ps = ctx.enter_context(tc.psum_pool(name="ps", bufs=1))
        ctx.enter_context(tc.manual_schedule())

        w_rows = w.rearrange("g (p j) m -> (g p) j m", j=PACK)
        dy_rows = dy.rearrange("g (p j) n -> (g p) j n", j=PACK)

        w_raw = sb.tile([P, PACK, M], F32, name="w_raw", align_bytes=64)
        dy_raw = [sb.tile([P, PACK, QUARTER], F32, name="dy_raw%d" % c, align_bytes=64) for c in range(4)]
        w_bf = sb.tile([P, M, PACK], BF16, name="w_bf", align_bytes=64)
        dy_bf = [sb.tile([P, QUARTER, PACK], BF16, name="dy_bf%d" % c, align_bytes=64) for c in range(4)]
        w_codes = sb.tile([P, M], U32, name="w_codes", align_bytes=64)
        w_scales = sb.tile([P, M], U8, name="w_scales", align_bytes=64)
        dy_codes = sb.tile([P, N], U32, name="dy_codes", align_bytes=64)
        dy_scales = sb.tile([P, N], U8, name="dy_scales", align_bytes=64)
        def pair_tiles(label):
            return [
                [sb.tile([P, 2, HALF], F32, name="%s%d%d" % (label, h, q), align_bytes=64) for q in range(2)]
                for h in range(2)
            ]

        gate = pair_tiles("gate")
        gated = pair_tiles("gated")
        slope = pair_tiles("slope")
        partial = pair_tiles("partial")
        result = pair_tiles("result")
        z = [[ps.tile([P, N], F32, name="z%d%d" % (h, g)) for g in range(G)] for h in range(2)]
        halves = [slice(0, HALF), slice(HALF, N)]

        def pair_rows(dram, h, q):
            return dram[2 * q : 2 * q + 2, :, halves[h]].rearrange("g m n -> m g n")

        quarters = [slice(c * QUARTER, (c + 1) * QUARTER) for c in range(4)]

        def load_dy(c):
            nc.sync.dma_start(out=dy_raw[c][:], in_=dy_rows[:, :, quarters[c]])

        def load_pair(tiles, dram, h, q):
            nc.sync.dma_start(out=tiles[h][q][:], in_=pair_rows(dram, h, q))

        nc.sync.dma_start(out=w_raw[:], in_=w_rows)
        load_dy(0)
        load_dy(1)
        load_pair(gate, sg, 0, 0)
        load_pair(gate, sg, 0, 1)
        load_dy(2)
        load_dy(3)
        load_pair(gated, xg, 0, 0)
        load_pair(gated, xg, 0, 1)
        load_pair(gate, sg, 1, 0)
        load_pair(gate, sg, 1, 1)
        load_pair(gated, xg, 1, 0)
        load_pair(gated, xg, 1, 1)

        def interleave(copy, dst, src, cols):
            copy(
                out=dst[:, cols, :].rearrange("p (c i) j -> p c j i", i=4),
                in_=src[:, :, cols].rearrange("p j (c i) -> p c j i", i=4),
            )

        def quantize(codes, scales, src):
            nc.vector.quantize_mx(
                out=codes.bitcast(E5M2X4), scales=scales, in_=src[:].rearrange("p c j -> p (c j)")
            )

        def quantize_dy(c):
            quantize(dy_codes[:, quarters[c]], dy_scales[:, quarters[c]], dy_bf[c])

        def multiply(h):
            for g in range(G):
                rows = slice(ROWS * g, ROWS * (g + 1))
                nc.tensor.matmul_mx(
                    out=z[h][g][:],
                    lhsT=w_codes[rows, :].bitcast(E5M2X4),
                    lhsT_scale=w_scales[rows, :],
                    rhs=dy_codes[rows, :].bitcast(E5M2X4),
                    rhs_scale=dy_scales[rows, :],
                    start=True,
                    stop=True,
                )

        def flat(t):
            return t[:].rearrange("p g n -> p (g n)")

        def make_slope(h, q):
            nc.vector.scalar_tensor_tensor(
                out=flat(slope[h][q]), in0=flat(gate[h][q]), scalar=1.0, in1=flat(gate[h][q]),
                op0=ALU.subtract, op1=ALU.mult,
            )

        def times_gated(h, q, members):
            nc.vector.tensor_tensor(
                out=result[h][q][:, members, :], in0=partial[h][q][:, members, :], in1=gated[h][q][:, members, :],
                op=ALU.mult,
            )
            nc.sync.dma_start(out=pair_rows(out, h, q)[:, members, :], in_=result[h][q][:, members, :])

        def times_sums(dst, src, h, g):
            q, i = divmod(g, 2)
            nc.vector.scalar_tensor_tensor(
                out=dst[h][q][:, i, :], in0=z[h][g][:, halves[h]], scalar=-1.0, in1=src[h][q][:, i, :],
                op0=ALU.mult, op1=ALU.mult,
            )

        nc.vector.memset(dy_codes[:, halves[1]], 0)
        nc.vector.memset(dy_scales[:, halves[1]].bitcast(U32), 0)
        interleave(nc.scalar.copy, w_bf, w_raw, slice(0, M))
        interleave(nc.vector.tensor_copy, dy_bf[0], dy_raw[0], slice(0, QUARTER))
        quantize(w_codes[:], w_scales[:], w_bf)
        quantize_dy(0)
        interleave(nc.vector.tensor_copy, dy_bf[1], dy_raw[1], slice(0, 72))
        interleave(nc.scalar.copy, dy_bf[1], dy_raw[1], slice(72, QUARTER))
        quantize_dy(1)
        multiply(0)
        for c in (2, 3):
            interleave(nc.scalar.copy, dy_bf[c], dy_raw[c], slice(0, QUARTER))

        for q in range(2):
            make_slope(0, q)
        for g in range(G):
            times_sums(partial, slope, 0, g)
        quantize_dy(2)
        times_gated(0, 0, slice(0, 2))
        quantize_dy(3)
        multiply(1)
        times_gated(0, 1, slice(0, 2))

        for q in range(2):
            make_slope(1, q)
        for g in range(G - 1):
            times_sums(partial, slope, 1, g)
        times_gated(1, 0, slice(0, 2))
        times_sums(partial, slope, 1, G - 1)
        times_gated(1, 1, slice(0, 1))
        times_gated(1, 1, slice(1, 2))
